import numpy as np
import ml_dtypes


def mxq(x, axis, fmt="e4m3"):
    dtype, down = {"e4m3": (ml_dtypes.float8_e4m3fn, 7), "e5m2": (ml_dtypes.float8_e5m2, 14)}[fmt]
    v = np.moveaxis(np.asarray(x, np.float32).astype(ml_dtypes.bfloat16).astype(np.float64), axis, -1)
    blocks = v.reshape(v.shape[:-1] + (-1, 32))
    amax = np.abs(blocks).max(-1, keepdims=True)
    byte = np.maximum(np.where(amax > 0, np.frexp(amax)[1] - 1 + 127, 0) - down, 1)
    scale = np.exp2(byte - 127.0)
    codes = (blocks / scale).astype(np.float32).astype(dtype).astype(np.float64)
    return np.moveaxis((codes * scale).reshape(v.shape), -1, axis)


WIDE = False


def mx_kscale(k):
    if not WIDE:
        return np.ones(k)
    levels = np.array([10, -10, 5, -5, 0])
    if k % 512:
        return np.exp2(np.random.permutation(np.resize(levels, k // 32))).repeat(32)
    a = np.empty((k // 512, 16))
    for p in range(k // 512):
        a[p, :8] = np.random.permutation(np.resize(levels, 8))
        for g in range(8):
            far = levels[np.abs(levels - a[p, g]) >= 10]
            a[p, g + 8] = far[np.random.randint(len(far))]
    return np.exp2(a.ravel()).repeat(32)


def f64(x):
    return np.asarray(x).astype(np.float64)


def striped(idx):
    return np.tile(np.asarray(idx).reshape(-1, 16).T, (8, 1)).astype(np.uint16)


def unstriped(offs):
    return offs[:16].T.reshape(-1).astype(np.int64)


E2M1 = np.array([0.0, 0.5, 1.0, 1.5, 2.0, 3.0, 4.0, 6.0, -0.0, -0.5, -1.0, -1.5, -2.0, -3.0, -4.0, -6.0])


def pack_weight(w, fmt):
    k, n = w.shape
    w = f64(np.asarray(w, np.float32).astype(ml_dtypes.bfloat16)).reshape(k // 32, 32, n)
    amax = np.abs(w).max(1)
    if fmt == "e4m3":
        byte = np.frexp(amax)[1] - 1 + 127 - 7
    else:
        mant, ex = np.frexp(amax / 6.0)
        byte = np.where(mant > 0.5, ex, ex - 1) + 127
    byte = np.clip(np.where(amax > 0, byte, 1), 1, 254)
    scaled = (w * np.exp2(127.0 - byte)[:, None, :]).reshape(k, n).astype(np.float32)
    by_word = np.ascontiguousarray(scaled.reshape(k // 512, 128, 4, n).transpose(0, 1, 3, 2))
    if fmt == "e4m3":
        words = by_word.astype(ml_dtypes.float8_e4m3fn).view(np.uint8)
    else:
        c = by_word.astype(ml_dtypes.float4_e2m1fn).view(np.uint8) & 0xF
        words = (c[..., 0::2] | (c[..., 1::2] << 4)).reshape(k // 512, 128, 2 * n)
    return np.ascontiguousarray(words), np.ascontiguousarray(byte.astype(np.uint8).reshape(k // 512, 16, n))


def unpack_weight(words, scales, fmt):
    g, _, n = scales.shape
    words = np.ascontiguousarray(words).reshape(g, 128, n, -1)
    if fmt == "e4m3":
        vals = words.view(ml_dtypes.float8_e4m3fn).astype(np.float64)
    else:
        nib = np.empty((g, 128, n, 4), np.uint8)
        nib[..., 0::2] = words & 0xF
        nib[..., 1::2] = words >> 4
        vals = E2M1[nib]
    vals = vals * np.repeat(np.exp2(scales.astype(np.float64) - 127.0), 8, axis=1)[..., None]
    return vals.transpose(0, 1, 3, 2).reshape(g * 512, n)


def bf(x):
    return np.asarray(x, np.float32).astype(ml_dtypes.bfloat16)


def planes(Y):
    r, m = Y.shape
    b = f64(bf(Y)).reshape(r // 32, 32, m)
    amax = np.abs(b).max(1)
    byte = np.clip(np.where(amax > 0, np.frexp(amax)[1] - 1 + 127 - 7, 1), 1, 254)
    codes = (b * np.exp2(127.0 - byte)[:, None, :]).reshape(r, m).astype(np.float32).astype(ml_dtypes.float8_e4m3fn).view(np.uint8)
    words = codes.reshape(r // 512, 128, 4, m).transpose(0, 1, 3, 2)
    return np.ascontiguousarray(words), np.ascontiguousarray(byte.astype(np.uint8).reshape(r // 512, 16, m))


B, N, T, D, NQ = 1, 512, 2048, 1024, 512


def setup_inputs():
    n = np.random.standard_normal
    idx = np.random.permutation(T)[:B * N]
    s = mx_kscale(D)[:, None]
    kp = pack_weight(n((D, T)) / s, "e2m1")
    return {
        "qT": (n((B, D, NQ)) * s * (1.00 / np.sqrt(D))).astype(np.float32),
        "k_words": np.ascontiguousarray(kp[0].reshape(1, 2, 128, T, 2).transpose(0, 2, 3, 1, 4)).reshape(1, 128, T, 4),
        "k_scales": kp[1],
        "ns": np.tile(np.random.uniform(0.2, 2.0, 2048), (128, 1)).astype(np.float32),
        "offs": striped(idx),
    }


def reference(qT, k_words, k_scales, ns, offs):
    idx = unstriped(offs)
    pick = lambda x, which: x[:, which].reshape(x.shape[0], B, -1).transpose(1, 0, 2)
    k = unpack_weight(k_words.reshape(1, 128, T, 2, 2).transpose(0, 3, 1, 2, 4).reshape(2, 128, 2 * T), k_scales, "e2m1")
    kg = pick(k, idx)
    qq = mxq(f64(qT), 1, "e4m3")
    a = kg.transpose(0, 2, 1) @ qq
    y = np.square(np.maximum(a, 0.0)) * pick(f64(ns), idx)[:, :1, :].transpose(0, 2, 1)
    Y = y[0]
    words, scales = planes(Y)
    return Y, words, scales

@@ -1,0 +1,171 @@
+from contextlib import ExitStack
+
+import concourse.mybir as mybir
+from concourse.masks import make_identity
+
+F32 = mybir.dt.float32
+BF16 = mybir.dt.bfloat16
+I32 = mybir.dt.int32
+U32 = mybir.dt.uint32
+U16 = mybir.dt.uint16
+U8 = mybir.dt.uint8
+FP8X4 = mybir.dt.float8_e4m3fn_x4
+FP4X4 = mybir.dt.float4_e2m1fn_x4
+ACT = mybir.ActivationFunctionType
+ALU = mybir.AluOpType
+
+P = 128
+SLOTS, NEURONS, D, NQ = 512, 2048, 1024, 512
+FLOPS = 2 * SLOTS * D * NQ
+BYTES = D * NQ * 4 + P * NEURONS * 4 + 32 * NEURONS + NEURONS * 4 + P * 32 * 2 + SLOTS * NQ * 5 + 16 * NQ
+
+CHUNKS = ((0, 128), (128, 384), (384, 512))
+LOADS = ((0, 0, 128), (1, 0, 128), (0, 128, 512), (1, 128, 384), (1, 384, 512))
+VECTOR_COLS = ((0, 0), (128, 128), (0, 64))
+Y_VECTOR_COLS = (128, 256, 128)
+
+
+def tile_attend_plh_relu2s_topk_kernel(tc, qT, k_words, k_scales, ns, offs, out_0, out_1, out_2):
+    nc = tc.nc
+    with ExitStack() as ctx:
+        keep = ctx.enter_context(tc.tile_pool(name="keep", bufs=1))
+        psum = ctx.enter_context(tc.psum_pool(name="psum", bufs=1))
+
+        offsets = keep.tile([P, SLOTS // 16], U16, name="offsets")
+        scale_table = keep.tile([P, NEURONS], U8, name="scale_table", tag="early", align_bytes=64)
+        ns_table = keep.tile([P, NEURONS], F32, name="ns_table", align_bytes=64)
+        word_table = keep.tile([P, NEURONS], U32, name="word_table", align_bytes=64)
+
+        nc.sync.dma_start(offsets[:], offs)
+        nc.sync.dma_start(scale_table[96:128, :].bitcast(I32), k_scales.bitcast(I32).rearrange("o f t -> f o t"))
+        nc.sync.dma_start(ns_table[127:128, :], ns[127:128, :])
+        q_raw = {}
+
+        def load_queries(loads, tile):
+            at = 0
+            for o, c0, c1 in loads:
+                raw = tile[:, at : at + 4 * (c1 - c0)].rearrange("p (t q) -> p t q", t=4)
+                at += 4 * (c1 - c0)
+                nc.sync.dma_start(raw, qT[0, 512 * o : 512 * (o + 1), c0:c1].rearrange("(p t) q -> p t q", t=4))
+                for c, (a, b) in enumerate(CHUNKS):
+                    if c0 <= a and b <= c1:
+                        q_raw[o, c] = raw[:, :, a - c0 : b - c0]
+
+        early, late = LOADS[:2], LOADS[2:]
+        q_early = keep.tile([P, sum(4 * (c1 - c0) for o, c0, c1 in early)], F32, name="q_early", align_bytes=64)
+        nc.sync.dma_start(word_table[:].bitcast(I32), k_words[0].rearrange("p t b -> p (t b)").bitcast(I32))
+        load_queries(early, q_early)
+
+        key_scales = keep.tile([P, 2 * SLOTS], U8, name="key_scales", align_bytes=64)
+        nc.vector.memset(scale_table[0:96, :].bitcast(I32), 0)
+        nc.vector.memset(key_scales[:].bitcast(I32), 0)
+        nc.vector.memset(ns_table[0:127, :], 0.0)
+        identity = keep.tile([P, P], F32, name="identity")
+        make_identity(nc, identity[:])
+
+        listed_scales = keep.tile([P, SLOTS], U8, name="listed_scales", align_bytes=64)
+        nc.vector.tensor_copy(listed_scales[:].rearrange("p (r s) -> p s r", r=4), scale_table[:].indirect(offsets[:]))
+        for quad in range(4):
+            nc.sync.dma_start(
+                key_scales[32 * quad : 32 * quad + 4, :].bitcast(I32).rearrange("p (o s) -> p o s", o=2),
+                listed_scales[96 + 8 * quad : 104 + 8 * quad, :].bitcast(I32),
+            )
+
+        q_late = keep.tile([P, sum(4 * (c1 - c0) for o, c0, c1 in late)], F32, name="q_late", tag="early", align_bytes=64)
+        load_queries(late, q_late)
+
+        listed_words = keep.tile([P, SLOTS], U32, name="listed_words", align_bytes=64)
+        nc.vector.tensor_copy(listed_words[:], word_table[:].indirect(offsets[:]))
+        keys = keep.tile([P, 2 * 2 * SLOTS], U8, name="keys", align_bytes=64)
+        nc.vector.tensor_copy(
+            keys[:].bitcast(U16).rearrange("p (o r a b) -> p o a r b", o=2, r=4, b=4),
+            listed_words[:].bitcast(U16).rearrange("p (a b r o) -> p o a r b", o=2, r=4, b=4),
+        )
+
+        listed_ns = keep.tile([P, SLOTS], F32, name="listed_ns", align_bytes=64)
+        nc.scalar.activation(listed_ns[:], ns_table[:].indirect(offsets[:]), ACT.Copy)
+        ns_turned = psum.tile([P, 4, P], F32, name="ns_turned")
+        for r in range(4):
+            nc.tensor.transpose(ns_turned[:, r, :], listed_ns[:, r:SLOTS:4], identity[:])
+        ns_cols = keep.tile([P, 4], F32, name="ns_cols")
+        nc.scalar.copy(ns_cols[:], ns_turned[:, :, 127])
+
+        def interleave(dst, src, width, on_vector):
+            for engine_copy, a, b in ((nc.vector.tensor_copy, 0, on_vector), (nc.scalar.copy, on_vector, width)):
+                if b > a:
+                    engine_copy(
+                        dst[:, 4 * a : 4 * b].rearrange("p (c i t) -> p c t i", i=4, t=4),
+                        src[:, :, a:b].rearrange("p t (c i) -> p c t i", i=4),
+                    )
+
+        banks = {}
+        y_scales = keep.tile([P, NQ], U8, name="y_scales", align_bytes=64)
+
+        def product(c, o):
+            a, b = CHUNKS[c]
+            w = b - a
+            q_bf = keep.tile([P, 4 * w], BF16, name="q_bf%d_%d" % (c, o), align_bytes=64)
+            interleave(q_bf, q_raw[o, c], w, VECTOR_COLS[c][o])
+            q_codes = keep.tile([P, w], U32, name="q_codes%d_%d" % (c, o), align_bytes=64)
+            q_scales = keep.tile([P, w], U8, name="q_scales%d_%d" % (c, o), align_bytes=64)
+            nc.vector.quantize_mx(out=q_codes[:].bitcast(FP8X4), scales=q_scales[:], in_=q_bf[:])
+            for r in range(4):
+                if o == 0 and r % 2 == 0:
+                    banks[c, r // 2] = psum.tile([P, 2, w], F32, name="bank%d_%d" % (c, r // 2))
+                col = SLOTS * o + P * r
+                nc.tensor.matmul_mx(
+                    out=banks[c, r // 2][:, r % 2, :],
+                    lhsT=keys[:, 2 * col : 2 * (col + P)].bitcast(FP4X4),
+                    lhsT_scale=key_scales[:, col : col + P],
+                    rhs=q_codes[:].bitcast(FP8X4),
+                    rhs_scale=q_scales[:],
+                    start=(o == 0 and r % 2 == 0),
+                    stop=(o == 1 and r % 2 == 1),
+                )
+
+        ys = {}
+
+        def activate(c):
+            a, b = CHUNKS[c]
+            w = b - a
+            y = keep.tile([P, 4, w], F32, name="y%d" % c, align_bytes=64)
+            ys[c] = y
+            for h in range(2):
+                relu = keep.tile([P, 2, w], F32, name="relu%d_%d" % (c, h), align_bytes=64)
+                nc.scalar.activation(relu[:], banks[c, h][:], ACT.Relu)
+                for j in range(2):
+                    r = 2 * h + j
+                    nc.vector.scalar_tensor_tensor(
+                        out=y[:, r, :], in0=relu[:, j, :], scalar=ns_cols[:, r : r + 1], in1=relu[:, j, :],
+                        op0=ALU.mult, op1=ALU.mult,
+                    )
+            nc.sync.dma_start(out_0.rearrange("(s r) q -> s r q", r=4)[:, :, a:b], y[:])
+
+        def hand_on(c):
+            a, b = CHUNKS[c]
+            w = b - a
+            y_bf = keep.tile([P, 4 * w], BF16, name="y_bf%d" % c, align_bytes=64)
+            interleave(y_bf, ys[c], w, Y_VECTOR_COLS[c])
+            y_codes = keep.tile([P, w], U32, name="y_codes%d" % c, align_bytes=64)
+            nc.vector.quantize_mx(out=y_codes[:].bitcast(FP8X4), scales=y_scales[:, a:b], in_=y_bf[:])
+            nc.sync.dma_start(
+                out_1[0].rearrange("p q u -> p (q u)")[:, 4 * a : 4 * b].bitcast(I32), y_codes[:].bitcast(I32)
+            )
+
+        product(0, 0)
+        product(0, 1)
+        product(1, 0)
+        activate(0)
+        product(2, 0)
+        hand_on(0)
+        product(1, 1)
+        product(2, 1)
+        activate(1)
+        activate(2)
+        hand_on(1)
+        hand_on(2)
+        for quad in range(4):
+            queue = nc.scalar if quad % 2 else nc.sync
+            queue.dma_start(
+                out_2[0, 4 * quad : 4 * quad + 4, :].bitcast(I32), y_scales[32 * quad : 32 * quad + 4, :].bitcast(I32)
+            )

@@ -15,14 +15,18 @@ ACT = mybir.ActivationFunctionType
 ALU = mybir.AluOpType
 
 P = 128
+PACK = 4
 SLOTS, NEURONS, D, NQ = 512, 2048, 1024, 512
-FLOPS = 2 * SLOTS * D * NQ
-BYTES = D * NQ * 4 + P * NEURONS * 4 + 32 * NEURONS + NEURONS * 4 + P * 32 * 2 + SLOTS * NQ * 5 + 16 * NQ
+K_PASS = P * PACK
+HALF = NQ // 2
+SCALE_ROW0 = 96
+NS_ROW = P - 1
 
-CHUNKS = ((0, 128), (128, 384), (384, 512))
-LOADS = ((0, 0, 128), (1, 0, 128), (0, 128, 512), (1, 128, 384), (1, 384, 512))
-VECTOR_COLS = ((0, 0), (128, 128), (0, 64))
-Y_VECTOR_COLS = (128, 256, 128)
+Q_ON_VECTOR = 160
+Y_ON_VECTOR = (64, 192)
+
+FLOPS = 2 * SLOTS * D * NQ
+BYTES = 4 * D * NQ + 4 * P * NEURONS + 32 * NEURONS + 4 * NEURONS + 2 * P * 32 + 5 * SLOTS * NQ + 16 * NQ
 
 
 def tile_attend_plh_relu2s_topk_kernel(tc, qT, k_words, k_scales, ns, offs, out_0, out_1, out_2):
@@ -31,139 +35,140 @@ def tile_attend_plh_relu2s_topk_kernel(tc, qT, k_words, k_scales, ns, offs, out_
         keep = ctx.enter_context(tc.tile_pool(name="keep", bufs=1))
         psum = ctx.enter_context(tc.psum_pool(name="psum", bufs=1))
 
-        offsets = keep.tile([P, SLOTS // 16], U16, name="offsets")
-        scale_table = keep.tile([P, NEURONS], U8, name="scale_table", tag="early", align_bytes=64)
-        ns_table = keep.tile([P, NEURONS], F32, name="ns_table", align_bytes=64)
-        word_table = keep.tile([P, NEURONS], U32, name="word_table", align_bytes=64)
+        def sbuf(name, shape, dtype, tag=None):
+            return keep.tile(shape, dtype, name=name, tag=tag or name, align_bytes=64)
 
+        def columns(half):
+            return slice(half * HALF, (half + 1) * HALF)
+
+        def query_rows(o):
+            return qT[0, K_PASS * o : K_PASS * (o + 1), :].rearrange("(p t) q -> p t q", t=PACK)
+
+        def round_and_interleave(dst, src, on_vector):
+            for copy, a, b in ((nc.vector.tensor_copy, 0, on_vector), (nc.scalar.copy, on_vector, HALF)):
+                copy(
+                    dst[:, PACK * a : PACK * b].rearrange("p (c i t) -> p c t i", i=4, t=PACK),
+                    src[:, :, a:b].rearrange("p t (c i) -> p c t i", i=4),
+                )
+
+        offsets = sbuf("offsets", [P, SLOTS // 16], U16)
+        scale_table = sbuf("scale_table", [P, NEURONS], U8)
+        ns_table = sbuf("ns_table", [P, NEURONS], F32)
+        word_table = sbuf("word_table", [P, NEURONS], U32)
+        q_pass0 = sbuf("q_pass0", [P, PACK, NQ], F32)
         nc.sync.dma_start(offsets[:], offs)
-        nc.sync.dma_start(scale_table[96:128, :].bitcast(I32), k_scales.bitcast(I32).rearrange("o f t -> f o t"))
-        nc.sync.dma_start(ns_table[127:128, :], ns[127:128, :])
-        q_raw = {}
-
-        def load_queries(loads, tile):
-            at = 0
-            for o, c0, c1 in loads:
-                raw = tile[:, at : at + 4 * (c1 - c0)].rearrange("p (t q) -> p t q", t=4)
-                at += 4 * (c1 - c0)
-                nc.sync.dma_start(raw, qT[0, 512 * o : 512 * (o + 1), c0:c1].rearrange("(p t) q -> p t q", t=4))
-                for c, (a, b) in enumerate(CHUNKS):
-                    if c0 <= a and b <= c1:
-                        q_raw[o, c] = raw[:, :, a - c0 : b - c0]
-
-        early, late = LOADS[:2], LOADS[2:]
-        q_early = keep.tile([P, sum(4 * (c1 - c0) for o, c0, c1 in early)], F32, name="q_early", align_bytes=64)
+        nc.sync.dma_start(scale_table[SCALE_ROW0:P, :].bitcast(I32), k_scales.bitcast(I32).rearrange("o f t -> f o t"))
+        nc.sync.dma_start(ns_table[NS_ROW:P, :], ns[NS_ROW:P, :])
         nc.sync.dma_start(word_table[:].bitcast(I32), k_words[0].rearrange("p t b -> p (t b)").bitcast(I32))
-        load_queries(early, q_early)
+        nc.sync.dma_start(q_pass0[:], query_rows(0))
 
-        key_scales = keep.tile([P, 2 * SLOTS], U8, name="key_scales", align_bytes=64)
-        nc.vector.memset(scale_table[0:96, :].bitcast(I32), 0)
+        key_scales = sbuf("key_scales", [P, 2 * SLOTS], U8)
+        nc.vector.memset(ns_table[0:NS_ROW, :], 0.0)
+        nc.vector.memset(scale_table[0:SCALE_ROW0, :].bitcast(I32), 0)
         nc.vector.memset(key_scales[:].bitcast(I32), 0)
-        nc.vector.memset(ns_table[0:127, :], 0.0)
-        identity = keep.tile([P, P], F32, name="identity")
+        identity = sbuf("identity", [P, P], F32)
         make_identity(nc, identity[:])
 
-        listed_scales = keep.tile([P, SLOTS], U8, name="listed_scales", align_bytes=64)
-        nc.vector.tensor_copy(listed_scales[:].rearrange("p (r s) -> p s r", r=4), scale_table[:].indirect(offsets[:]))
+        listed_scales = sbuf("listed_scales", [P, SLOTS], U8)
+        nc.vector.tensor_copy(
+            listed_scales[:].rearrange("p (r s) -> p s r", r=PACK), scale_table[:].indirect(offsets[:])
+        )
         for quad in range(4):
+            first = SCALE_ROW0 + 8 * quad
             nc.sync.dma_start(
                 key_scales[32 * quad : 32 * quad + 4, :].bitcast(I32).rearrange("p (o s) -> p o s", o=2),
-                listed_scales[96 + 8 * quad : 104 + 8 * quad, :].bitcast(I32),
+                listed_scales[first : first + 8, :].bitcast(I32),
             )
 
-        q_late = keep.tile([P, sum(4 * (c1 - c0) for o, c0, c1 in late)], F32, name="q_late", tag="early", align_bytes=64)
-        load_queries(late, q_late)
+        q_pass1 = sbuf("q_pass1", [P, 2 * PACK * HALF], F32, tag="scale_table")
+        q_raw = {}
+        for half in range(2):
+            q_raw[0, half] = q_pass0[:, :, columns(half)]
+            q_raw[1, half] = q_pass1[:, PACK * HALF * half : PACK * HALF * (half + 1)].rearrange(
+                "p (t q) -> p t q", t=PACK
+            )
+            nc.sync.dma_start(q_raw[1, half], query_rows(1)[:, :, columns(half)])
 
-        listed_words = keep.tile([P, SLOTS], U32, name="listed_words", align_bytes=64)
+        listed_words = sbuf("listed_words", [P, SLOTS], U32)
         nc.vector.tensor_copy(listed_words[:], word_table[:].indirect(offsets[:]))
-        keys = keep.tile([P, 2 * 2 * SLOTS], U8, name="keys", align_bytes=64)
+        keys = sbuf("keys", [P, 2 * 2 * SLOTS], U8)
         nc.vector.tensor_copy(
-            keys[:].bitcast(U16).rearrange("p (o r a b) -> p o a r b", o=2, r=4, b=4),
-            listed_words[:].bitcast(U16).rearrange("p (a b r o) -> p o a r b", o=2, r=4, b=4),
+            keys[:].bitcast(U16).rearrange("p (o r a b) -> p o a r b", o=2, r=PACK, b=4),
+            listed_words[:].bitcast(U16).rearrange("p (a b r o) -> p o a r b", o=2, r=PACK, b=4),
         )
 
-        listed_ns = keep.tile([P, SLOTS], F32, name="listed_ns", align_bytes=64)
+        listed_ns = sbuf("listed_ns", [P, SLOTS], F32)
         nc.scalar.activation(listed_ns[:], ns_table[:].indirect(offsets[:]), ACT.Copy)
-        ns_turned = psum.tile([P, 4, P], F32, name="ns_turned")
-        for r in range(4):
-            nc.tensor.transpose(ns_turned[:, r, :], listed_ns[:, r:SLOTS:4], identity[:])
-        ns_cols = keep.tile([P, 4], F32, name="ns_cols")
-        nc.scalar.copy(ns_cols[:], ns_turned[:, :, 127])
+        ns_turned = psum.tile([P, PACK, P], F32, name="ns_turned", tag="sums1_3")
+        for r in range(PACK):
+            nc.tensor.transpose(ns_turned[:, r, :], listed_ns[:, r:SLOTS:PACK], identity[:])
+        ns_cols = sbuf("ns_cols", [P, PACK], F32)
+        nc.scalar.copy(ns_cols[:], ns_turned[:, :, NS_ROW])
 
-        def interleave(dst, src, width, on_vector):
-            for engine_copy, a, b in ((nc.vector.tensor_copy, 0, on_vector), (nc.scalar.copy, on_vector, width)):
-                if b > a:
-                    engine_copy(
-                        dst[:, 4 * a : 4 * b].rearrange("p (c i t) -> p c t i", i=4, t=4),
-                        src[:, :, a:b].rearrange("p t (c i) -> p c t i", i=4),
-                    )
+        sums, relus, ys = {}, {}, {}
+        y_codes = sbuf("y_codes", [P, NQ], U32)
+        y_scales = sbuf("y_scales", [P, NQ], U8)
 
-        banks = {}
-        y_scales = keep.tile([P, NQ], U8, name="y_scales", align_bytes=64)
-
-        def product(c, o):
-            a, b = CHUNKS[c]
-            w = b - a
-            q_bf = keep.tile([P, 4 * w], BF16, name="q_bf%d_%d" % (c, o), align_bytes=64)
-            interleave(q_bf, q_raw[o, c], w, VECTOR_COLS[c][o])
-            q_codes = keep.tile([P, w], U32, name="q_codes%d_%d" % (c, o), align_bytes=64)
-            q_scales = keep.tile([P, w], U8, name="q_scales%d_%d" % (c, o), align_bytes=64)
+        def multiply(half, o):
+            q_bf = sbuf("q_bf%d_%d" % (half, o), [P, PACK * HALF], BF16)
+            round_and_interleave(q_bf, q_raw[o, half], Q_ON_VECTOR)
+            q_codes = sbuf("q_codes%d_%d" % (half, o), [P, HALF], U32)
+            q_scales = sbuf("q_scales%d_%d" % (half, o), [P, HALF], U8)
             nc.vector.quantize_mx(out=q_codes[:].bitcast(FP8X4), scales=q_scales[:], in_=q_bf[:])
-            for r in range(4):
-                if o == 0 and r % 2 == 0:
-                    banks[c, r // 2] = psum.tile([P, 2, w], F32, name="bank%d_%d" % (c, r // 2))
+            for r in range(PACK):
+                if o == 0:
+                    name = "sums%d_%d" % (half, r)
+                    sums[half, r] = psum.tile([P, HALF], F32, name=name, tag=name)
                 col = SLOTS * o + P * r
                 nc.tensor.matmul_mx(
-                    out=banks[c, r // 2][:, r % 2, :],
+                    out=sums[half, r][:],
                     lhsT=keys[:, 2 * col : 2 * (col + P)].bitcast(FP4X4),
                     lhsT_scale=key_scales[:, col : col + P],
                     rhs=q_codes[:].bitcast(FP8X4),
                     rhs_scale=q_scales[:],
-                    start=(o == 0 and r % 2 == 0),
-                    stop=(o == 1 and r % 2 == 1),
+                    start=(o == 0),
+                    stop=(o == 1),
                 )
 
-        ys = {}
+        def rectify(half):
+            for r in range(PACK):
+                relus[half, r] = sbuf("relu%d_%d" % (half, r), [P, HALF], F32)
+                nc.scalar.activation(relus[half, r][:], sums[half, r][:], ACT.Relu)
 
-        def activate(c):
-            a, b = CHUNKS[c]
-            w = b - a
-            y = keep.tile([P, 4, w], F32, name="y%d" % c, align_bytes=64)
-            ys[c] = y
-            for h in range(2):
-                relu = keep.tile([P, 2, w], F32, name="relu%d_%d" % (c, h), align_bytes=64)
-                nc.scalar.activation(relu[:], banks[c, h][:], ACT.Relu)
-                for j in range(2):
-                    r = 2 * h + j
-                    nc.vector.scalar_tensor_tensor(
-                        out=y[:, r, :], in0=relu[:, j, :], scalar=ns_cols[:, r : r + 1], in1=relu[:, j, :],
-                        op0=ALU.mult, op1=ALU.mult,
+        def square(half):
+            ys[half] = sbuf("y%d" % half, [P, PACK, HALF], F32)
+            for r in range(PACK):
+                nc.vector.scalar_tensor_tensor(
+                    out=ys[half][:, r, :],
+                    in0=relus[half, r][:],
+                    scalar=ns_cols[:, r : r + 1],
+                    in1=relus[half, r][:],
+                    op0=ALU.mult,
+                    op1=ALU.mult,
+                )
+                if r % 2 == 1:
+                    nc.sync.dma_start(
+                        out_0.rearrange("(s r) q -> s r q", r=PACK)[:, r - 1 : r + 1, columns(half)],
+                        ys[half][:, r - 1 : r + 1, :],
                     )
-            nc.sync.dma_start(out_0.rearrange("(s r) q -> s r q", r=4)[:, :, a:b], y[:])
 
-        def hand_on(c):
-            a, b = CHUNKS[c]
-            w = b - a
-            y_bf = keep.tile([P, 4 * w], BF16, name="y_bf%d" % c, align_bytes=64)
-            interleave(y_bf, ys[c], w, Y_VECTOR_COLS[c])
-            y_codes = keep.tile([P, w], U32, name="y_codes%d" % c, align_bytes=64)
-            nc.vector.quantize_mx(out=y_codes[:].bitcast(FP8X4), scales=y_scales[:, a:b], in_=y_bf[:])
-            nc.sync.dma_start(
-                out_1[0].rearrange("p q u -> p (q u)")[:, 4 * a : 4 * b].bitcast(I32), y_codes[:].bitcast(I32)
-            )
+        def hand_on(half, tag):
+            y_bf = sbuf("y_bf%d" % half, [P, PACK * HALF], BF16, tag=tag)
+            round_and_interleave(y_bf, ys[half], Y_ON_VECTOR[half])
+            cols = columns(half)
+            nc.vector.quantize_mx(out=y_codes[:, cols].bitcast(FP8X4), scales=y_scales[:, cols], in_=y_bf[:])
+            nc.sync.dma_start(out_1[0, :, cols, :].rearrange("p q u -> p (q u)").bitcast(I32), y_codes[:, cols].bitcast(I32))
 
-        product(0, 0)
-        product(0, 1)
-        product(1, 0)
-        activate(0)
-        product(2, 0)
-        hand_on(0)
-        product(1, 1)
-        product(2, 1)
-        activate(1)
-        activate(2)
-        hand_on(1)
-        hand_on(2)
+        multiply(0, 0)
+        multiply(0, 1)
+        rectify(0)
+        multiply(1, 0)
+        multiply(1, 1)
+        square(0)
+        rectify(1)
+        square(1)
+        hand_on(0, "relu1_0")
+        hand_on(1, None)
         for quad in range(4):
             queue = nc.scalar if quad % 2 else nc.sync
             queue.dma_start(

@@ -22,7 +22,7 @@ HALF = NQ // 2
 SCALE_ROW0 = 96
 NS_ROW = P - 1
 
-Q_ON_VECTOR = 160
+Q_ON_VECTOR = ((160, 160), (96, 160))
 Y_ON_VECTOR = (64, 192)
 
 FLOPS = 2 * SLOTS * D * NQ
@@ -102,19 +102,19 @@ def tile_attend_plh_relu2s_topk_kernel(tc, qT, k_words, k_scales, ns, offs, out_
         ns_turned = psum.tile([P, PACK, P], F32, name="ns_turned", tag="sums1_3")
         for r in range(PACK):
             nc.tensor.transpose(ns_turned[:, r, :], listed_ns[:, r:SLOTS:PACK], identity[:])
-        ns_cols = sbuf("ns_cols", [P, PACK], F32)
-        nc.scalar.copy(ns_cols[:], ns_turned[:, :, NS_ROW])
 
-        sums, relus, ys = {}, {}, {}
+        q_codes, q_scales, sums, relus, ys = {}, {}, {}, {}, {}
         y_codes = sbuf("y_codes", [P, NQ], U32)
         y_scales = sbuf("y_scales", [P, NQ], U8)
 
-        def multiply(half, o):
+        def quantise(half, o):
             q_bf = sbuf("q_bf%d_%d" % (half, o), [P, PACK * HALF], BF16)
-            round_and_interleave(q_bf, q_raw[o, half], Q_ON_VECTOR)
-            q_codes = sbuf("q_codes%d_%d" % (half, o), [P, HALF], U32)
-            q_scales = sbuf("q_scales%d_%d" % (half, o), [P, HALF], U8)
-            nc.vector.quantize_mx(out=q_codes[:].bitcast(FP8X4), scales=q_scales[:], in_=q_bf[:])
+            round_and_interleave(q_bf, q_raw[o, half], Q_ON_VECTOR[half][o])
+            q_codes[half, o] = sbuf("q_codes%d_%d" % (half, o), [P, HALF], U32)
+            q_scales[half, o] = sbuf("q_scales%d_%d" % (half, o), [P, HALF], U8)
+            nc.vector.quantize_mx(out=q_codes[half, o][:].bitcast(FP8X4), scales=q_scales[half, o][:], in_=q_bf[:])
+
+        def multiply(half, o):
             for r in range(PACK):
                 if o == 0:
                     name = "sums%d_%d" % (half, r)
@@ -124,8 +124,8 @@ def tile_attend_plh_relu2s_topk_kernel(tc, qT, k_words, k_scales, ns, offs, out_
                     out=sums[half, r][:],
                     lhsT=keys[:, 2 * col : 2 * (col + P)].bitcast(FP4X4),
                     lhsT_scale=key_scales[:, col : col + P],
-                    rhs=q_codes[:].bitcast(FP8X4),
-                    rhs_scale=q_scales[:],
+                    rhs=q_codes[half, o][:].bitcast(FP8X4),
+                    rhs_scale=q_scales[half, o][:],
                     start=(o == 0),
                     stop=(o == 1),
                 )
@@ -135,7 +135,7 @@ def tile_attend_plh_relu2s_topk_kernel(tc, qT, k_words, k_scales, ns, offs, out_
                 relus[half, r] = sbuf("relu%d_%d" % (half, r), [P, HALF], F32)
                 nc.scalar.activation(relus[half, r][:], sums[half, r][:], ACT.Relu)
 
-        def square(half):
+        def square(half, ns_cols):
             ys[half] = sbuf("y%d" % half, [P, PACK, HALF], F32)
             for r in range(PACK):
                 nc.vector.scalar_tensor_tensor(
@@ -159,14 +159,19 @@ def tile_attend_plh_relu2s_topk_kernel(tc, qT, k_words, k_scales, ns, offs, out_
             nc.vector.quantize_mx(out=y_codes[:, cols].bitcast(FP8X4), scales=y_scales[:, cols], in_=y_bf[:])
             nc.sync.dma_start(out_1[0, :, cols, :].rearrange("p q u -> p (q u)").bitcast(I32), y_codes[:, cols].bitcast(I32))
 
-        multiply(0, 0)
-        multiply(0, 1)
+        for o in range(2):
+            quantise(0, o)
+            multiply(0, o)
         rectify(0)
+        quantise(1, 0)
+        ns_cols = sbuf("ns_cols", [P, PACK], F32, tag="q_pass0")
+        nc.scalar.copy(ns_cols[:], ns_turned[:, :, NS_ROW])
         multiply(1, 0)
+        quantise(1, 1)
         multiply(1, 1)
-        square(0)
+        square(0, ns_cols)
         rectify(1)
-        square(1)
+        square(1, ns_cols)
         hand_on(0, "relu1_0")
         hand_on(1, None)
         for quad in range(4):

from contextlib import ExitStack

import concourse.mybir as mybir
from concourse.masks import make_identity

F32 = mybir.dt.float32
BF16 = mybir.dt.bfloat16
I32 = mybir.dt.int32
U32 = mybir.dt.uint32
U16 = mybir.dt.uint16
U8 = mybir.dt.uint8
FP8X4 = mybir.dt.float8_e4m3fn_x4
FP4X4 = mybir.dt.float4_e2m1fn_x4
ACT = mybir.ActivationFunctionType
ALU = mybir.AluOpType

P = 128
PACK = 4
SLOTS, NEURONS, D, NQ = 512, 2048, 1024, 512
K_PASS = P * PACK
HALF = NQ // 2
SCALE_ROW0 = 96
NS_ROW = P - 1

Q_ON_VECTOR = ((160, 160), (96, 160))
Y_ON_VECTOR = (64, 192)

FLOPS = 2 * SLOTS * D * NQ
BYTES = 4 * D * NQ + 4 * P * NEURONS + 32 * NEURONS + 4 * NEURONS + 2 * P * 32 + 5 * SLOTS * NQ + 16 * NQ


def tile_attend_plh_relu2s_topk_kernel(tc, qT, k_words, k_scales, ns, offs, out_0, out_1, out_2):
    nc = tc.nc
    with ExitStack() as ctx:
        keep = ctx.enter_context(tc.tile_pool(name="keep", bufs=1))
        psum = ctx.enter_context(tc.psum_pool(name="psum", bufs=1))

        def sbuf(name, shape, dtype, tag=None):
            return keep.tile(shape, dtype, name=name, tag=tag or name, align_bytes=64)

        def columns(half):
            return slice(half * HALF, (half + 1) * HALF)

        def query_rows(o):
            return qT[0, K_PASS * o : K_PASS * (o + 1), :].rearrange("(p t) q -> p t q", t=PACK)

        def round_and_interleave(dst, src, on_vector):
            for copy, a, b in ((nc.vector.tensor_copy, 0, on_vector), (nc.scalar.copy, on_vector, HALF)):
                copy(
                    dst[:, PACK * a : PACK * b].rearrange("p (c i t) -> p c t i", i=4, t=PACK),
                    src[:, :, a:b].rearrange("p t (c i) -> p c t i", i=4),
                )

        offsets = sbuf("offsets", [P, SLOTS // 16], U16)
        scale_table = sbuf("scale_table", [P, NEURONS], U8)
        ns_table = sbuf("ns_table", [P, NEURONS], F32)
        word_table = sbuf("word_table", [P, NEURONS], U32)
        q_pass0 = sbuf("q_pass0", [P, PACK, NQ], F32)
        nc.sync.dma_start(offsets[:], offs)
        nc.sync.dma_start(scale_table[SCALE_ROW0:P, :].bitcast(I32), k_scales.bitcast(I32).rearrange("o f t -> f o t"))
        nc.sync.dma_start(ns_table[NS_ROW:P, :], ns[NS_ROW:P, :])
        nc.sync.dma_start(word_table[:].bitcast(I32), k_words[0].rearrange("p t b -> p (t b)").bitcast(I32))
        nc.sync.dma_start(q_pass0[:], query_rows(0))

        key_scales = sbuf("key_scales", [P, 2 * SLOTS], U8)
        nc.vector.memset(ns_table[0:NS_ROW, :], 0.0)
        nc.vector.memset(scale_table[0:SCALE_ROW0, :].bitcast(I32), 0)
        nc.vector.memset(key_scales[:].bitcast(I32), 0)
        identity = sbuf("identity", [P, P], F32)
        make_identity(nc, identity[:])

        listed_scales = sbuf("listed_scales", [P, SLOTS], U8)
        nc.vector.tensor_copy(
            listed_scales[:].rearrange("p (r s) -> p s r", r=PACK), scale_table[:].indirect(offsets[:])
        )
        for quad in range(4):
            first = SCALE_ROW0 + 8 * quad
            nc.sync.dma_start(
                key_scales[32 * quad : 32 * quad + 4, :].bitcast(I32).rearrange("p (o s) -> p o s", o=2),
                listed_scales[first : first + 8, :].bitcast(I32),
            )

        q_pass1 = sbuf("q_pass1", [P, 2 * PACK * HALF], F32, tag="scale_table")
        q_raw = {}
        for half in range(2):
            q_raw[0, half] = q_pass0[:, :, columns(half)]
            q_raw[1, half] = q_pass1[:, PACK * HALF * half : PACK * HALF * (half + 1)].rearrange(
                "p (t q) -> p t q", t=PACK
            )
            nc.sync.dma_start(q_raw[1, half], query_rows(1)[:, :, columns(half)])

        listed_words = sbuf("listed_words", [P, SLOTS], U32)
        nc.vector.tensor_copy(listed_words[:], word_table[:].indirect(offsets[:]))
        keys = sbuf("keys", [P, 2 * 2 * SLOTS], U8)
        nc.vector.tensor_copy(
            keys[:].bitcast(U16).rearrange("p (o r a b) -> p o a r b", o=2, r=PACK, b=4),
            listed_words[:].bitcast(U16).rearrange("p (a b r o) -> p o a r b", o=2, r=PACK, b=4),
        )

        listed_ns = sbuf("listed_ns", [P, SLOTS], F32)
        nc.scalar.activation(listed_ns[:], ns_table[:].indirect(offsets[:]), ACT.Copy)
        ns_turned = psum.tile([P, PACK, P], F32, name="ns_turned", tag="sums1_3")
        for r in range(PACK):
            nc.tensor.transpose(ns_turned[:, r, :], listed_ns[:, r:SLOTS:PACK], identity[:])

        q_codes, q_scales, sums, relus, ys = {}, {}, {}, {}, {}
        y_codes = sbuf("y_codes", [P, NQ], U32)
        y_scales = sbuf("y_scales", [P, NQ], U8)

        def quantise(half, o):
            q_bf = sbuf("q_bf%d_%d" % (half, o), [P, PACK * HALF], BF16)
            round_and_interleave(q_bf, q_raw[o, half], Q_ON_VECTOR[half][o])
            q_codes[half, o] = sbuf("q_codes%d_%d" % (half, o), [P, HALF], U32)
            q_scales[half, o] = sbuf("q_scales%d_%d" % (half, o), [P, HALF], U8)
            nc.vector.quantize_mx(out=q_codes[half, o][:].bitcast(FP8X4), scales=q_scales[half, o][:], in_=q_bf[:])

        def multiply(half, o):
            for r in range(PACK):
                if o == 0:
                    name = "sums%d_%d" % (half, r)
                    sums[half, r] = psum.tile([P, HALF], F32, name=name, tag=name)
                col = SLOTS * o + P * r
                nc.tensor.matmul_mx(
                    out=sums[half, r][:],
                    lhsT=keys[:, 2 * col : 2 * (col + P)].bitcast(FP4X4),
                    lhsT_scale=key_scales[:, col : col + P],
                    rhs=q_codes[half, o][:].bitcast(FP8X4),
                    rhs_scale=q_scales[half, o][:],
                    start=(o == 0),
                    stop=(o == 1),
                )

        def rectify(half):
            for r in range(PACK):
                relus[half, r] = sbuf("relu%d_%d" % (half, r), [P, HALF], F32)
                nc.scalar.activation(relus[half, r][:], sums[half, r][:], ACT.Relu)

        def square(half, ns_cols):
            ys[half] = sbuf("y%d" % half, [P, PACK, HALF], F32)
            for r in range(PACK):
                nc.vector.scalar_tensor_tensor(
                    out=ys[half][:, r, :],
                    in0=relus[half, r][:],
                    scalar=ns_cols[:, r : r + 1],
                    in1=relus[half, r][:],
                    op0=ALU.mult,
                    op1=ALU.mult,
                )
                if r % 2 == 1:
                    nc.sync.dma_start(
                        out_0.rearrange("(s r) q -> s r q", r=PACK)[:, r - 1 : r + 1, columns(half)],
                        ys[half][:, r - 1 : r + 1, :],
                    )

        def hand_on(half, tag):
            y_bf = sbuf("y_bf%d" % half, [P, PACK * HALF], BF16, tag=tag)
            round_and_interleave(y_bf, ys[half], Y_ON_VECTOR[half])
            cols = columns(half)
            nc.vector.quantize_mx(out=y_codes[:, cols].bitcast(FP8X4), scales=y_scales[:, cols], in_=y_bf[:])
            nc.sync.dma_start(out_1[0, :, cols, :].rearrange("p q u -> p (q u)").bitcast(I32), y_codes[:, cols].bitcast(I32))

        for o in range(2):
            quantise(0, o)
            multiply(0, o)
        rectify(0)
        quantise(1, 0)
        ns_cols = sbuf("ns_cols", [P, PACK], F32, tag="q_pass0")
        nc.scalar.copy(ns_cols[:], ns_turned[:, :, NS_ROW])
        multiply(1, 0)
        quantise(1, 1)
        multiply(1, 1)
        square(0, ns_cols)
        rectify(1)
        square(1, ns_cols)
        hand_on(0, "relu1_0")
        hand_on(1, None)
        for quad in range(4):
            queue = nc.scalar if quad % 2 else nc.sync
            queue.dma_start(
                out_2[0, 4 * quad : 4 * quad + 4, :].bitcast(I32), y_scales[32 * quad : 32 * quad + 4, :].bitcast(I32)
            )
